import numpy as np
import ml_dtypes


def mxq(x, axis, fmt="e4m3"):
    dtype, down = {"e4m3": (ml_dtypes.float8_e4m3fn, 7), "e5m2": (ml_dtypes.float8_e5m2, 14)}[fmt]
    v = np.moveaxis(np.asarray(x, np.float32).astype(ml_dtypes.bfloat16).astype(np.float64), axis, -1)
    blocks = v.reshape(v.shape[:-1] + (-1, 32))
    amax = np.abs(blocks).max(-1, keepdims=True)
    byte = np.maximum(np.where(amax > 0, np.frexp(amax)[1] - 1 + 127, 0) - down, 1)
    scale = np.exp2(byte - 127.0)
    codes = (blocks / scale).astype(np.float32).astype(dtype).astype(np.float64)
    return np.moveaxis((codes * scale).reshape(v.shape), -1, axis)


WIDE = False


def mx_kscale(k):
    if not WIDE:
        return np.ones(k)
    levels = np.array([10, -10, 5, -5, 0])
    if k % 512:
        return np.exp2(np.random.permutation(np.resize(levels, k // 32))).repeat(32)
    a = np.empty((k // 512, 16))
    for p in range(k // 512):
        a[p, :8] = np.random.permutation(np.resize(levels, 8))
        for g in range(8):
            far = levels[np.abs(levels - a[p, g]) >= 10]
            a[p, g + 8] = far[np.random.randint(len(far))]
    return np.exp2(a.ravel()).repeat(32)


def f64(x):
    return np.asarray(x).astype(np.float64)


def striped(idx):
    return np.tile(idx.reshape(-1, 16).T, (8, 1)).astype(np.uint16)


def unstriped(offs):
    return offs[:16].T.reshape(-1).astype(np.int64)


def striped8(idx):
    return np.concatenate([x.reshape(-1, 16).T for x in idx]).astype(np.uint16)


def runs(offs, k):
    lists = np.stack([offs[16 * r : 16 * r + 16].T.reshape(-1) for r in range(8)]).astype(np.int64)
    return lists[np.arange(k) % 512 // 64]


def pack_weight(w):
    k, n = w.shape
    w = f64(np.asarray(w, np.float32).astype(ml_dtypes.bfloat16)).reshape(k // 32, 32, n)
    amax = np.abs(w).max(1)
    byte = np.clip(np.where(amax > 0, np.frexp(amax)[1] - 1 + 127 - 7, 1), 1, 254)
    scaled = (w * np.exp2(127.0 - byte)[:, None, :]).reshape(k, n).astype(np.float32)
    words = np.ascontiguousarray(scaled.reshape(k // 512, 128, 4, n).transpose(0, 1, 3, 2)).astype(ml_dtypes.float8_e4m3fn).view(np.uint8)
    return words, np.ascontiguousarray(byte.astype(np.uint8).reshape(k // 512, 16, n))


def unpack_weight(words, scales):
    g, p, n, _ = words.shape
    vals = np.ascontiguousarray(words).view(ml_dtypes.float8_e4m3fn).astype(np.float64) * np.repeat(np.exp2(scales.astype(np.float64) - 127.0), 8, axis=1)[..., None]
    return vals.transpose(0, 1, 3, 2).reshape(g * 512, n)


E2M1 = np.array([0.0, 0.5, 1.0, 1.5, 2.0, 3.0, 4.0, 6.0, -0.0, -0.5, -1.0, -1.5, -2.0, -3.0, -4.0, -6.0])


def pack_fp4(w):
    k, n = w.shape
    w = f64(np.asarray(w, np.float32).astype(ml_dtypes.bfloat16)).reshape(k // 32, 32, n)
    amax = np.abs(w).max(1)
    mant, ex = np.frexp(amax / 6.0)
    byte = np.clip(np.where(amax > 0, np.where(mant > 0.5, ex, ex - 1) + 127, 1), 1, 254)
    scaled = (w * np.exp2(127.0 - byte)[:, None, :]).reshape(k, n).astype(np.float32)
    c = np.ascontiguousarray(scaled.reshape(k // 512, 128, 4, n).transpose(0, 1, 3, 2)).astype(ml_dtypes.float4_e2m1fn).view(np.uint8) & 0xF
    words = (c[..., 0::2] | (c[..., 1::2] << 4)).reshape(k // 512, 128, 2 * n)
    return np.ascontiguousarray(words), np.ascontiguousarray(byte.astype(np.uint8).reshape(k // 512, 16, n))


def unpack_fp4(words, scales):
    g, _, n = scales.shape
    words = np.ascontiguousarray(words).reshape(g, 128, n, 2)
    nib = np.empty((g, 128, n, 4), np.uint8)
    nib[..., 0::2] = words & 0xF
    nib[..., 1::2] = words >> 4
    vals = E2M1[nib] * np.repeat(np.exp2(scales.astype(np.float64) - 127.0), 8, axis=1)[..., None]
    return vals.transpose(0, 1, 3, 2).reshape(g * 512, n)


def sigmoid(v):
    return 1.0 / (1.0 + np.exp(-np.maximum(v, -700.0)))

def planes(y):
    n, m = y.shape
    v = y.astype(np.float32).astype(ml_dtypes.bfloat16).astype(np.float64).reshape(n // 32, 32, m)
    top = np.abs(v).max(1)
    byte = np.clip(np.where(top > 0, np.frexp(top)[1] - 1 + 127 - 7, 1), 1, 254)
    codes = (v * np.exp2(127.0 - byte)[:, None, :]).reshape(n, m).astype(np.float32).astype(ml_dtypes.float8_e4m3fn).view(np.uint8)
    words = codes.reshape(n // 512, 128, 4, m).transpose(0, 1, 3, 2)
    return np.ascontiguousarray(words), np.ascontiguousarray(byte.astype(np.uint8).reshape(n // 512, 16, m))


K, T, S, N, H, J = 512, 2048, 512, 512, 512, 512


def setup_inputs():
    n = np.random.standard_normal
    s = mx_kscale(K)[:, None]
    u = mx_kscale(H)
    packed_xT = pack_weight(n((K, T)) * s)
    packed_w1 = pack_fp4(n((K, H)) / np.sqrt(K) / s)
    packed_w2 = pack_fp4(n((H, N)) / np.sqrt(2 * H) / u[:, None])
    packed_w3 = pack_fp4(n((K, N)) / np.sqrt(2 * K) / s)
    return {
        "x_words": packed_xT[0],
        "x_scales": packed_xT[1],
        "w1_words": packed_w1[0],
        "w1_scales": packed_w1[1],
        "tau": np.random.uniform(0.3, 0.9, (H, 1)).astype(np.float32),
        "tau2": np.random.uniform(0.3, 0.9, (H, 1)).astype(np.float32),
        "gn": (np.random.uniform(0.5, 1.5, (H, 1)) * u[:, None]).astype(np.float32),
        "w2_words": packed_w2[0],
        "w2_scales": packed_w2[1],
        "w3_words": packed_w3[0],
        "w3_scales": packed_w3[1],
        "tab": n((N, J)).astype(np.float32),
        "sl": np.random.uniform(1.0, 2.0, (N, 1)).astype(np.float32),
        "th": (0.5 * n((N, 1))).astype(np.float32),
        "offs": striped8(np.random.randint(0, T, (8, S))),
        "n1": striped8(np.stack([np.random.permutation(S) for _ in range(8)])),
        "n2": striped8(np.stack([np.random.permutation(S) for _ in range(8)])),
        "two": striped(np.random.permutation(T)[:S]),
        "n3": striped(np.random.randint(0, J, S)),
        "n4": striped(np.random.permutation(S)),
    }


def reference(x_words, x_scales, w1_words, w1_scales, tau, tau2, gn, w2_words, w2_scales, w3_words, w3_scales, tab, sl, th, offs, n1, n2, two, n3, n4):
    xq = unpack_weight(x_words, x_scales)[np.arange(K)[:, None], runs(offs, K)]
    y = unpack_fp4(w1_words, w1_scales).T @ xq
    top = y.max(axis=1, keepdims=True)
    ea = np.exp(f64(tau) * (y[np.arange(H)[:, None], runs(n1, H)] - top))
    ea2 = np.exp(f64(tau2) * (y[np.arange(H)[:, None], runs(n2, H)] - top))
    z = f64(gn) * (0.5 * y + np.log((ea + 0.25) / (ea2 + 0.25)))
    x_two = unpack_weight(x_words, x_scales)[:, unstriped(two)]
    h = unpack_fp4(w2_words, w2_scales).T @ mxq(z, 0, "e4m3") + unpack_fp4(w3_words, w3_scales).T @ x_two
    sg = sigmoid(f64(sl) * (f64(tab)[:, unstriped(n3)] - f64(th)))
    out_0 = h * sg - (0.5 * h[:, unstriped(n4)])
    return (out_0,) + planes(out_0)

@@ -1,0 +1,247 @@
+from contextlib import ExitStack
+
+import concourse.mybir as mybir
+
+F32 = mybir.dt.float32
+BF16 = mybir.dt.bfloat16
+I32 = mybir.dt.int32
+U32 = mybir.dt.uint32
+U16 = mybir.dt.uint16
+U8 = mybir.dt.uint8
+FP8X4 = mybir.dt.float8_e4m3fn_x4
+FP4X4 = mybir.dt.float4_e2m1fn_x4
+ALU = mybir.AluOpType
+ACT = mybir.ActivationFunctionType
+
+P = 128
+T = 2048
+S = 512
+HALF = 256
+F32_LOWEST = -3.4028234663852886e38
+FLOPS = 3 * 2 * 512 * 512 * 512
+SCALAR_TILES = (2, 3)
+
+
+def tile_picked_hmixeosekd_none_po_kernel(
+    tc, x_words, x_scales, w1_words, w1_scales, tau, tau2, gn, w2_words, w2_scales, w3_words, w3_scales,
+    tab, sl, th, offs, n1, n2, two, n3, n4, out_0, out_1, out_2,
+):
+    nc = tc.nc
+    with ExitStack() as ctx:
+        lists = ctx.enter_context(tc.tile_pool(name="lists", bufs=1))
+        sb = ctx.enter_context(tc.tile_pool(name="sb", bufs=1))
+        ps = ctx.enter_context(tc.psum_pool(name="ps", bufs=1))
+        halves = [slice(h * HALF, (h + 1) * HALF) for h in range(2)]
+        list_halves = [slice(h * HALF // 16, (h + 1) * HALF // 16) for h in range(2)]
+
+        def load_list(name, src):
+            tile = lists.tile([P, S // 16], U16, name=name)
+            nc.sync.dma_start(tile[:], src)
+            return tile
+
+        def load_columns(tile, srcs, queue):
+            for i, src in enumerate(srcs):
+                queue.dma_start(tile[:, i, 0:4], src.rearrange("(p t) o -> p (t o)", t=4))
+
+        def load_scale_rows(src, queues):
+            for r in range(4):
+                queues[r].dma_start(ws_raw[r:P:32, :].bitcast(I32), src[0, r:16:4, :].bitcast(I32))
+
+        def deal_scales(name):
+            dealt = sb.tile([P, S], U8, name=name, align_bytes=64)
+            nc.vector.tensor_copy(
+                out=dealt[:].rearrange("p (t m) -> p t m", t=4),
+                in_=ws_raw[:].rearrange("p (m t) -> p t m", t=4),
+            )
+            return dealt
+
+        def deal_words_vector(name):
+            dealt = sb.tile([P, 2 * S], U8, name=name, align_bytes=64)
+            nc.vector.tensor_copy(
+                out=dealt[:].rearrange("p (t m b) -> p t m b", t=4, b=2),
+                in_=ww_raw[:].rearrange("p (m t b) -> p t m b", t=4, b=2),
+            )
+            return dealt
+
+        def gather_scales(name, offsets, queues):
+            picked = sb.tile([P, S], U8, name=name + "_picked", tag="picked")
+            nc.vector.tensor_copy(picked[:], xs_win[:].indirect(offsets[:]))
+            plane = sb.tile([P, S], U8, name=name + "_plane", align_bytes=64)
+            nc.vector.tensor_copy(plane[:].bitcast(I32), picked[:].bitcast(I32))
+            for r in range(1, 4):
+                queues[r - 1].dma_start(plane[r:P:32, :].bitcast(I32), picked[8 * r : P : 32, :].bitcast(I32))
+            return plane
+
+        xs_win = sb.tile([P, T], U8, name="xs_win")
+        nc.gpsimd.memset(xs_win[:].bitcast(I32), 0)
+        ws_raw = sb.tile([P, S], U8, name="ws_raw")
+        nc.vector.memset(ws_raw[:].bitcast(I32), 0)
+        offs_t = load_list("offs_t", offs)
+        nc.scalar.dma_start(xs_win[0:P:8, :].bitcast(I32), x_scales[0].bitcast(I32))
+        n1_t = load_list("n1_t", n1)
+        n2_t = load_list("n2_t", n2)
+        two_t = load_list("two_t", two)
+        n3_t = load_list("n3_t", n3)
+        n4_t = load_list("n4_t", n4)
+        xw_win = sb.tile([P, T], I32, name="xw_win")
+        nc.sync.dma_start(xw_win[:], x_words[0].rearrange("p n t -> p (n t)").bitcast(I32))
+        ww_raw = sb.tile([P, 2 * S], U8, name="ww_raw")
+        nc.gpsimd.dma_start(ww_raw[:].bitcast(I32), w1_words[0].bitcast(I32))
+        load_scale_rows(w1_scales, (nc.scalar, nc.scalar, nc.scalar, nc.gpsimd))
+        rates = sb.tile([P, 2, 8], F32, name="rates")
+        load_columns(rates, (tau, tau2), nc.gpsimd)
+
+        xs_plane = gather_scales("xs", offs_t, (nc.sync, nc.scalar, nc.sync))
+        w1_d = sb.tile([P, 2 * S], U8, name="w1_d", align_bytes=64)
+        nc.scalar.copy(
+            out=w1_d[:].bitcast(U16).rearrange("p (t m) -> p t m", t=4),
+            in_=ww_raw[:].bitcast(U16).rearrange("p (m t) -> p t m", t=4),
+        )
+        w1_s = deal_scales("w1_s")
+        xq = sb.tile([P, S], U32, name="xq", align_bytes=64)
+        for h in range(2):
+            nc.vector.tensor_copy(xq[:, halves[h]], xw_win[:].bitcast(U32).indirect(offs_t[:, list_halves[h]]))
+
+
+        def mx(out, w_d, w_s, t, rhs, rhs_s, start, stop):
+            nc.tensor.matmul_mx(
+                out=out, lhsT=w_d[:, 256 * t : 256 * (t + 1)].bitcast(FP4X4), lhsT_scale=w_s[:, P * t : P * (t + 1)],
+                rhs=rhs.bitcast(FP8X4), rhs_scale=rhs_s, start=start, stop=stop,
+            )
+
+        y_t, bias_t = [], []
+        for t in range(4):
+            bank = ps.tile([P, S], F32, name="y_bank%d" % t)
+            if t == 0:
+                for cols in halves:
+                    mx(bank[:, cols], w1_d, w1_s, t, xq[:, cols], xs_plane[:, cols], True, True)
+            else:
+                mx(bank[:], w1_d, w1_s, t, xq[:], xs_plane[:], True, True)
+            y = sb.tile([P, S], F32, name="y%d" % t, tag="row%d" % t)
+            top = sb.tile([P, 1], F32, name="top%d" % t)
+            nc.vector.tensor_scalar(y[:], bank[:], 1.0, F32_LOWEST, ALU.mult, ALU.max, accum_out=top[:])
+            bias = sb.tile([P, 2], F32, name="bias%d" % t)
+            nc.vector.tensor_scalar(bias[:], rates[:, :, t], top[:], -1.0, ALU.mult, ALU.mult)
+            y_t.append(y)
+            bias_t.append(bias)
+
+        ea = [sb.tile([P, 8, HALF], F32, name="ea%d" % h, align_bytes=64) for h in range(2)]
+        for t in range(4):
+            for l, lst in enumerate((n1_t, n2_t)):
+                for h in range(2):
+                    nc.scalar.activation(
+                        ea[h][:, 2 * t + l, :], y_t[t][:].indirect(lst[:, list_halves[h]]),
+                        ACT.Exp, bias=bias_t[t][:, l : l + 1], scale=rates[:, l, t : t + 1],
+                    )
+
+        x2s_plane = gather_scales("x2s", two_t, [nc.sync] * 3)
+        ww_raw = sb.tile([P, 2 * S], U8, name="ww_late", tag="xq", align_bytes=64)
+        nc.sync.dma_start(ww_raw[:].bitcast(I32), w3_words[0].bitcast(I32))
+        load_scale_rows(w3_scales, [nc.sync] * 4)
+        late = sb.tile([P, 3, 8], F32, name="late", tag="picked")
+        load_columns(late, (gn, sl, th), nc.sync)
+        gn_t, sl_t, th_t = late[:, 0, 0:4], late[:, 1, 0:4], late[:, 2, 0:4]
+        w3_d = deal_words_vector("w3_d")
+        w3_s = deal_scales("w3_s")
+        nc.sync.dma_start(ww_raw[:].bitcast(I32), w2_words[0].bitcast(I32))
+        load_scale_rows(w2_scales, [nc.sync] * 4)
+        x2q = sb.tile([P, S], U32, name="x2q", align_bytes=64)
+        nc.vector.tensor_copy(x2q[:], xw_win[:].bitcast(U32).indirect(two_t[:]))
+        gains = sb.tile([P, 2, 4], F32, name="gains")
+        nc.vector.tensor_scalar(gains[:, 0, :], gn_t, 0.5, None, ALU.mult)
+        nc.vector.tensor_scalar(gains[:, 1, :], gn_t, -1.0, None, ALU.mult)
+        yg = sb.tile([P, 4, S], F32, name="yg")
+        for t in range(4):
+            nc.vector.tensor_scalar(yg[:, t, :], y_t[t][:], gains[:, 0, t : t + 1], None, ALU.mult)
+        w2_d = deal_words_vector("w2_d")
+        w2_s = deal_scales("w2_s")
+        sg_bias = sb.tile([P, 4], F32, name="sg_bias")
+        nc.vector.scalar_tensor_tensor(sg_bias[:], sl_t, -1.0, th_t, ALU.mult, ALU.mult)
+        h_bank = [ps.tile([P, S], F32, name="h_bank%d" % t) for t in range(4)]
+        for t in range(4):
+            mx(h_bank[t][:], w3_d, w3_s, t, x2q[:], x2s_plane[:], True, False)
+        tab_t = []
+        for t in range(4):
+            tile = sb.tile([P, S], F32, name="tab%d" % t, tag="row%d" % t)
+            nc.sync.dma_start(tile[:], tab.rearrange("(p t) c -> p t c", t=4)[:, t, :])
+            tab_t.append(tile)
+
+        ln = [sb.tile([P, 8, HALF], F32, name="ln%d" % h) for h in range(2)]
+        zb = [sb.tile([P, 4, HALF], BF16, name="zb%d" % h) for h in range(2)]
+        part = [sb.tile([P, 4, HALF], F32, name="part%d" % h) for h in range(2)]
+        for h in range(2):
+            for t in range(4):
+                nc.scalar.activation(ln[h][:, 2 * t : 2 * t + 2, :], ea[h][:, 2 * t : 2 * t + 2, :], ACT.Ln, bias=0.25)
+        for h in range(2):
+            for step in range(5):
+                if step < 4:
+                    t = step
+                    nc.vector.scalar_tensor_tensor(
+                        part[h][:, t, :], ln[h][:, 2 * t, :], gn_t[:, t : t + 1], yg[:, t, halves[h]], ALU.mult, ALU.add
+                    )
+                if step > 0:
+                    t = step - 1
+                    nc.vector.scalar_tensor_tensor(
+                        zb[h][:, t, :], ln[h][:, 2 * t + 1, :], gains[:, 1, t : t + 1], part[h][:, t, :], ALU.mult, ALU.add
+                    )
+
+        def interleave(engine_copy, dst, src):
+            engine_copy(
+                out=dst.rearrange("p (c i) t -> p c t i", i=4), in_=src.rearrange("p t (c i) -> p c t i", i=4)
+            )
+
+        zi = [
+            sb.tile([P, HALF, 4], BF16, name="zi0", tag="ea1", align_bytes=64),
+            sb.tile([P, HALF, 4], BF16, name="zi1", align_bytes=64),
+        ]
+        zq = [sb.tile([P, HALF], U32, name="zq%d" % h, align_bytes=64) for h in range(2)]
+        zs = [sb.tile([P, HALF], U8, name="zs%d" % h, align_bytes=64) for h in range(2)]
+        interleave(nc.scalar.copy, zi[0][:], zb[0][:])
+        interleave(nc.vector.tensor_copy, zi[1][:], zb[1][:])
+        for h in range(2):
+            nc.vector.quantize_mx(out=zq[h][:].bitcast(FP8X4), scales=zs[h][:], in_=zi[h][:].rearrange("p c t -> p (c t)"))
+        for h in range(2):
+            for t in range(4):
+                mx(h_bank[t][:, halves[h]], w2_d, w2_s, t, zq[h][:], zs[h][:], False, h == 1)
+
+        sg = sb.tile([P, 4, S], F32, name="sg", tag="zb0")
+        for t in range(4):
+            for h in range(2):
+                nc.scalar.activation(
+                    sg[:, t, halves[h]], tab_t[t][:].indirect(n3_t[:, list_halves[h]]),
+                    ACT.Sigmoid, bias=sg_bias[:, t : t + 1], scale=sl_t[:, t : t + 1],
+                )
+
+        hs = [sb.tile([P, S], F32, name="hs%d" % t) for t in range(4)]
+        prod = sb.tile([P, 4, S], F32, name="prod")
+        fetched = sb.tile([P, 4, S], F32, name="fetched")
+        res = [sb.tile([P, 4, HALF], F32, name="res%d" % h) for h in range(2)]
+        rb = [sb.tile([P, HALF, 4], BF16, name="rb%d" % h, align_bytes=64) for h in range(2)]
+        oq = sb.tile([P, S], U32, name="oq", align_bytes=64)
+        osc = sb.tile([P, S], U8, name="osc", align_bytes=64)
+        out_rows = out_0.rearrange("(p t) c -> p t c", t=4)
+        out_words = out_1[0].rearrange("p c r -> p (c r)").bitcast(I32)
+
+        for t in range(4):
+            nc.vector.tensor_scalar(hs[t][:], h_bank[t][:], -0.5, None, ALU.mult)
+        for t in range(4):
+            nc.vector.tensor_tensor(prod[:, t, :], h_bank[t][:], sg[:, t, :], ALU.mult)
+            if t not in SCALAR_TILES:
+                for h in range(2):
+                    looked = hs[t][:].indirect(n4_t[:, list_halves[h]])
+                    nc.vector.tensor_tensor(res[h][:, t, :], looked, prod[:, t, halves[h]], ALU.add)
+        for h in range(2):
+            for t in SCALAR_TILES:
+                nc.scalar.activation(fetched[:, t, halves[h]], hs[t][:].indirect(n4_t[:, list_halves[h]]), ACT.Copy)
+                nc.vector.tensor_tensor(res[h][:, t, :], fetched[:, t, halves[h]], prod[:, t, halves[h]], ALU.add)
+            nc.sync.dma_start(out_rows[:, :, halves[h]], res[h][:])
+        interleave(nc.scalar.copy, rb[0][:], res[0][:])
+        interleave(nc.vector.tensor_copy, rb[1][:], res[1][:])
+        for h in (1, 0):
+            nc.vector.quantize_mx(
+                out=oq[:, halves[h]].bitcast(FP8X4), scales=osc[:, halves[h]], in_=rb[h][:].rearrange("p c t -> p (c t)")
+            )
+            nc.sync.dma_start(out_words[:, halves[h]], oq[:, halves[h]].bitcast(I32))
+        for q in range(4):
+            queue = nc.scalar if q % 2 == 0 else nc.sync
+            queue.dma_start(out_2[0, 4 * q : 4 * q + 4, :].bitcast(I32), osc[32 * q : 32 * q + 4, :].bitcast(I32))

@@ -19,6 +19,7 @@ S = 512
 HALF = 256
 F32_LOWEST = -3.4028234663852886e38
 FLOPS = 3 * 2 * 512 * 512 * 512
+DIVIDED = False
 SCALAR_TILES = (2, 3)
 
 
@@ -74,8 +75,6 @@ def tile_picked_hmixeosekd_none_po_kernel(
 
         xs_win = sb.tile([P, T], U8, name="xs_win")
         nc.gpsimd.memset(xs_win[:].bitcast(I32), 0)
-        ws_raw = sb.tile([P, S], U8, name="ws_raw")
-        nc.vector.memset(ws_raw[:].bitcast(I32), 0)
         offs_t = load_list("offs_t", offs)
         nc.scalar.dma_start(xs_win[0:P:8, :].bitcast(I32), x_scales[0].bitcast(I32))
         n1_t = load_list("n1_t", n1)
@@ -87,11 +86,13 @@ def tile_picked_hmixeosekd_none_po_kernel(
         nc.sync.dma_start(xw_win[:], x_words[0].rearrange("p n t -> p (n t)").bitcast(I32))
         ww_raw = sb.tile([P, 2 * S], U8, name="ww_raw")
         nc.gpsimd.dma_start(ww_raw[:].bitcast(I32), w1_words[0].bitcast(I32))
-        load_scale_rows(w1_scales, (nc.scalar, nc.scalar, nc.scalar, nc.gpsimd))
+        ws_raw = sb.tile([P, S], U8, name="ws_raw")
+        nc.gpsimd.memset(ws_raw[:].bitcast(I32), 0)
+        load_scale_rows(w1_scales, [nc.sync] * 4)
         rates = sb.tile([P, 2, 8], F32, name="rates")
         load_columns(rates, (tau, tau2), nc.gpsimd)
 
-        xs_plane = gather_scales("xs", offs_t, (nc.sync, nc.scalar, nc.sync))
+        xs_plane = gather_scales("xs", offs_t, [nc.sync] * 3)
         w1_d = sb.tile([P, 2 * S], U8, name="w1_d", align_bytes=64)
         nc.scalar.copy(
             out=w1_d[:].bitcast(U16).rearrange("p (t m) -> p t m", t=4),
@@ -109,7 +110,11 @@ def tile_picked_hmixeosekd_none_po_kernel(
                 rhs=rhs.bitcast(FP8X4), rhs_scale=rhs_s, start=start, stop=stop,
             )
 
-        y_t, bias_t = [], []
+        wide = [sb.tile([P, 2 * S], F32, name="wide%d" % t) for t in range(4)]
+        hs = [sb.tile([P, S if t in SCALAR_TILES else 2 * S], F32, name="hs%d" % t) for t in range(4)]
+        for tile in wide + [hs[t] for t in range(4) if t not in SCALAR_TILES]:
+            nc.vector.memset(tile[:, S:], 0.0)
+        bias_t = []
         for t in range(4):
             bank = ps.tile([P, S], F32, name="y_bank%d" % t)
             if t == 0:
@@ -117,22 +122,19 @@ def tile_picked_hmixeosekd_none_po_kernel(
                     mx(bank[:, cols], w1_d, w1_s, t, xq[:, cols], xs_plane[:, cols], True, True)
             else:
                 mx(bank[:], w1_d, w1_s, t, xq[:], xs_plane[:], True, True)
-            y = sb.tile([P, S], F32, name="y%d" % t, tag="row%d" % t)
             top = sb.tile([P, 1], F32, name="top%d" % t)
-            nc.vector.tensor_scalar(y[:], bank[:], 1.0, F32_LOWEST, ALU.mult, ALU.max, accum_out=top[:])
+            nc.vector.tensor_scalar(wide[t][:, :S], bank[:], 1.0, F32_LOWEST, ALU.mult, ALU.max, accum_out=top[:])
             bias = sb.tile([P, 2], F32, name="bias%d" % t)
             nc.vector.tensor_scalar(bias[:], rates[:, :, t], top[:], -1.0, ALU.mult, ALU.mult)
-            y_t.append(y)
             bias_t.append(bias)
 
-        ea = [sb.tile([P, 8, HALF], F32, name="ea%d" % h, align_bytes=64) for h in range(2)]
+        ea = [sb.tile([P, 2, S], F32, name="ea%d" % t) for t in range(4)]
         for t in range(4):
-            for l, lst in enumerate((n1_t, n2_t)):
-                for h in range(2):
-                    nc.scalar.activation(
-                        ea[h][:, 2 * t + l, :], y_t[t][:].indirect(lst[:, list_halves[h]]),
-                        ACT.Exp, bias=bias_t[t][:, l : l + 1], scale=rates[:, l, t : t + 1],
-                    )
+            for l, lst in ((1, n2_t), (0, n1_t)):
+                nc.scalar.activation(
+                    ea[t][:, l, :], wide[t][:].indirect(lst[:]),
+                    ACT.Exp, bias=bias_t[t][:, l : l + 1], scale=rates[:, l, t : t + 1],
+                )
 
         x2s_plane = gather_scales("x2s", two_t, [nc.sync] * 3)
         ww_raw = sb.tile([P, 2 * S], U8, name="ww_late", tag="xq", align_bytes=64)
@@ -145,14 +147,22 @@ def tile_picked_hmixeosekd_none_po_kernel(
         w3_s = deal_scales("w3_s")
         nc.sync.dma_start(ww_raw[:].bitcast(I32), w2_words[0].bitcast(I32))
         load_scale_rows(w2_scales, [nc.sync] * 4)
+        ratio = sb.tile([P, S], F32, name="ratio")
+        if DIVIDED:
+            below = sb.tile([P, S], F32, name="below")
+            inverse = sb.tile([P, S], F32, name="inverse")
+            nc.vector.tensor_scalar(below[:], ea[0][:, 1, :], 0.25, None, ALU.add)
+            nc.vector.reciprocal(inverse[:], below[:])
         x2q = sb.tile([P, S], U32, name="x2q", align_bytes=64)
         nc.vector.tensor_copy(x2q[:], xw_win[:].bitcast(U32).indirect(two_t[:]))
+        if DIVIDED:
+            nc.vector.scalar_tensor_tensor(ratio[:], ea[0][:, 0, :], 0.25, inverse[:], ALU.add, ALU.mult)
         gains = sb.tile([P, 2, 4], F32, name="gains")
         nc.vector.tensor_scalar(gains[:, 0, :], gn_t, 0.5, None, ALU.mult)
         nc.vector.tensor_scalar(gains[:, 1, :], gn_t, -1.0, None, ALU.mult)
         yg = sb.tile([P, 4, S], F32, name="yg")
         for t in range(4):
-            nc.vector.tensor_scalar(yg[:, t, :], y_t[t][:], gains[:, 0, t : t + 1], None, ALU.mult)
+            nc.vector.tensor_scalar(yg[:, t, :], wide[t][:, :S], gains[:, 0, t : t + 1], None, ALU.mult)
         w2_d = deal_words_vector("w2_d")
         w2_s = deal_scales("w2_s")
         sg_bias = sb.tile([P, 4], F32, name="sg_bias")
@@ -160,62 +170,51 @@ def tile_picked_hmixeosekd_none_po_kernel(
         h_bank = [ps.tile([P, S], F32, name="h_bank%d" % t) for t in range(4)]
         for t in range(4):
             mx(h_bank[t][:], w3_d, w3_s, t, x2q[:], x2s_plane[:], True, False)
-        tab_t = []
         for t in range(4):
-            tile = sb.tile([P, S], F32, name="tab%d" % t, tag="row%d" % t)
-            nc.sync.dma_start(tile[:], tab.rearrange("(p t) c -> p t c", t=4)[:, t, :])
-            tab_t.append(tile)
+            nc.sync.dma_start(wide[t][:, :S], tab.rearrange("(p t) c -> p t c", t=4)[:, t, :])
 
-        ln = [sb.tile([P, 8, HALF], F32, name="ln%d" % h) for h in range(2)]
-        zb = [sb.tile([P, 4, HALF], BF16, name="zb%d" % h) for h in range(2)]
-        part = [sb.tile([P, 4, HALF], F32, name="part%d" % h) for h in range(2)]
-        for h in range(2):
-            for t in range(4):
-                nc.scalar.activation(ln[h][:, 2 * t : 2 * t + 2, :], ea[h][:, 2 * t : 2 * t + 2, :], ACT.Ln, bias=0.25)
-        for h in range(2):
-            for step in range(5):
-                if step < 4:
-                    t = step
-                    nc.vector.scalar_tensor_tensor(
-                        part[h][:, t, :], ln[h][:, 2 * t, :], gn_t[:, t : t + 1], yg[:, t, halves[h]], ALU.mult, ALU.add
-                    )
-                if step > 0:
-                    t = step - 1
-                    nc.vector.scalar_tensor_tensor(
-                        zb[h][:, t, :], ln[h][:, 2 * t + 1, :], gains[:, 1, t : t + 1], part[h][:, t, :], ALU.mult, ALU.add
-                    )
+        ln = sb.tile([P, 4, 2, S], F32, name="ln")
+        zb = sb.tile([P, 4, S], BF16, name="zb")
+        part = sb.tile([P, 4, S], F32, name="part")
+        twice = [1, 2, 3] if DIVIDED else [0, 1, 2, 3]
+        for l in range(2):
+            nc.scalar.activation(ln[:, twice[0], l, :], ea[twice[0]][:, l, :], ACT.Ln, bias=0.25)
+        for t in twice[1:]:
+            nc.scalar.activation(ln[:, t, :, :], ea[t][:], ACT.Ln, bias=0.25)
+        if DIVIDED:
+            nc.scalar.activation(ln[:, 0, 0, :], ratio[:], ACT.Ln)
+        for t in twice:
+            nc.vector.scalar_tensor_tensor(part[:, t, :], ln[:, t, 0, :], gn_t[:, t : t + 1], yg[:, t, :], ALU.mult, ALU.add)
+            nc.vector.scalar_tensor_tensor(zb[:, t, :], ln[:, t, 1, :], gains[:, 1, t : t + 1], part[:, t, :], ALU.mult, ALU.add)
+        if DIVIDED:
+            nc.vector.scalar_tensor_tensor(zb[:, 0, :], ln[:, 0, 0, :], gn_t[:, 0:1], yg[:, 0, :], ALU.mult, ALU.add)
 
         def interleave(engine_copy, dst, src):
             engine_copy(
                 out=dst.rearrange("p (c i) t -> p c t i", i=4), in_=src.rearrange("p t (c i) -> p c t i", i=4)
             )
 
-        zi = [
-            sb.tile([P, HALF, 4], BF16, name="zi0", tag="ea1", align_bytes=64),
-            sb.tile([P, HALF, 4], BF16, name="zi1", align_bytes=64),
-        ]
+        zi = [sb.tile([P, HALF, 4], BF16, name="zi%d" % h, align_bytes=64) for h in range(2)]
         zq = [sb.tile([P, HALF], U32, name="zq%d" % h, align_bytes=64) for h in range(2)]
         zs = [sb.tile([P, HALF], U8, name="zs%d" % h, align_bytes=64) for h in range(2)]
-        interleave(nc.scalar.copy, zi[0][:], zb[0][:])
-        interleave(nc.vector.tensor_copy, zi[1][:], zb[1][:])
+        for h in range(2):
+            interleave(nc.vector.tensor_copy, zi[h][:], zb[:, :, halves[h]])
         for h in range(2):
             nc.vector.quantize_mx(out=zq[h][:].bitcast(FP8X4), scales=zs[h][:], in_=zi[h][:].rearrange("p c t -> p (c t)"))
-        for h in range(2):
-            for t in range(4):
-                mx(h_bank[t][:, halves[h]], w2_d, w2_s, t, zq[h][:], zs[h][:], False, h == 1)
-
-        sg = sb.tile([P, 4, S], F32, name="sg", tag="zb0")
         for t in range(4):
             for h in range(2):
-                nc.scalar.activation(
-                    sg[:, t, halves[h]], tab_t[t][:].indirect(n3_t[:, list_halves[h]]),
-                    ACT.Sigmoid, bias=sg_bias[:, t : t + 1], scale=sl_t[:, t : t + 1],
-                )
+                mx(h_bank[t][:, halves[h]], w2_d, w2_s, t, zq[h][:], zs[h][:], False, h == 1)
 
-        hs = [sb.tile([P, S], F32, name="hs%d" % t) for t in range(4)]
+        sg = sb.tile([P, 4, S], F32, name="sg", tag="ratio" if DIVIDED else "ea3")
+        for t in range(4):
+            nc.scalar.activation(
+                sg[:, t, :], wide[t][:].indirect(n3_t[:]),
+                ACT.Sigmoid, bias=sg_bias[:, t : t + 1], scale=sl_t[:, t : t + 1],
+            )
+
         prod = sb.tile([P, 4, S], F32, name="prod")
         fetched = sb.tile([P, 4, S], F32, name="fetched")
-        res = [sb.tile([P, 4, HALF], F32, name="res%d" % h) for h in range(2)]
+        res = sb.tile([P, 4, S], F32, name="res")
         rb = [sb.tile([P, HALF, 4], BF16, name="rb%d" % h, align_bytes=64) for h in range(2)]
         oq = sb.tile([P, S], U32, name="oq", align_bytes=64)
         osc = sb.tile([P, S], U8, name="osc", align_bytes=64)
@@ -223,20 +222,22 @@ def tile_picked_hmixeosekd_none_po_kernel(
         out_words = out_1[0].rearrange("p c r -> p (c r)").bitcast(I32)
 
         for t in range(4):
-            nc.vector.tensor_scalar(hs[t][:], h_bank[t][:], -0.5, None, ALU.mult)
-        for t in range(4):
+            if t in SCALAR_TILES:
+                nc.scalar.activation(hs[t][:], h_bank[t][:], ACT.Copy, scale=-0.5)
+            else:
+                nc.vector.tensor_scalar(hs[t][:, :S], h_bank[t][:], -0.5, None, ALU.mult)
             nc.vector.tensor_tensor(prod[:, t, :], h_bank[t][:], sg[:, t, :], ALU.mult)
             if t not in SCALAR_TILES:
-                for h in range(2):
-                    looked = hs[t][:].indirect(n4_t[:, list_halves[h]])
-                    nc.vector.tensor_tensor(res[h][:, t, :], looked, prod[:, t, halves[h]], ALU.add)
+                nc.vector.tensor_tensor(res[:, t, :], hs[t][:].indirect(n4_t[:]), prod[:, t, :], ALU.add)
+                nc.sync.dma_start(out_rows[:, t, :], res[:, t, :])
         for h in range(2):
             for t in SCALAR_TILES:
                 nc.scalar.activation(fetched[:, t, halves[h]], hs[t][:].indirect(n4_t[:, list_halves[h]]), ACT.Copy)
-                nc.vector.tensor_tensor(res[h][:, t, :], fetched[:, t, halves[h]], prod[:, t, halves[h]], ALU.add)
-            nc.sync.dma_start(out_rows[:, :, halves[h]], res[h][:])
-        interleave(nc.scalar.copy, rb[0][:], res[0][:])
-        interleave(nc.vector.tensor_copy, rb[1][:], res[1][:])
+                nc.vector.tensor_tensor(res[:, t, halves[h]], fetched[:, t, halves[h]], prod[:, t, halves[h]], ALU.add)
+        for t in SCALAR_TILES:
+            nc.sync.dma_start(out_rows[:, t, :], res[:, t, :])
+        interleave(nc.scalar.copy, rb[0][:], res[:, :, halves[0]])
+        interleave(nc.vector.tensor_copy, rb[1][:], res[:, :, halves[1]])
         for h in (1, 0):
             nc.vector.quantize_mx(
                 out=oq[:, halves[h]].bitcast(FP8X4), scales=osc[:, halves[h]], in_=rb[h][:].rearrange("p c t -> p (c t)")

@@ -19,7 +19,7 @@ S = 512
 HALF = 256
 F32_LOWEST = -3.4028234663852886e38
 FLOPS = 3 * 2 * 512 * 512 * 512
-DIVIDED = False
+DIVIDED = True
 SCALAR_TILES = (2, 3)
 
 
@@ -111,9 +111,9 @@ def tile_picked_hmixeosekd_none_po_kernel(
             )
 
         wide = [sb.tile([P, 2 * S], F32, name="wide%d" % t) for t in range(4)]
-        hs = [sb.tile([P, S if t in SCALAR_TILES else 2 * S], F32, name="hs%d" % t) for t in range(4)]
-        for tile in wide + [hs[t] for t in range(4) if t not in SCALAR_TILES]:
-            nc.vector.memset(tile[:, S:], 0.0)
+        hs = [sb.tile([P, S], F32, name="hs%d" % t) for t in range(4)]
+        for tile in wide:
+            nc.gpsimd.memset(tile[:, S:], 0.0)
         bias_t = []
         for t in range(4):
             bank = ps.tile([P, S], F32, name="y_bank%d" % t)
@@ -137,10 +137,9 @@ def tile_picked_hmixeosekd_none_po_kernel(
                 )
 
         x2s_plane = gather_scales("x2s", two_t, [nc.sync] * 3)
-        ww_raw = sb.tile([P, 2 * S], U8, name="ww_late", tag="xq", align_bytes=64)
         nc.sync.dma_start(ww_raw[:].bitcast(I32), w3_words[0].bitcast(I32))
         load_scale_rows(w3_scales, [nc.sync] * 4)
-        late = sb.tile([P, 3, 8], F32, name="late", tag="picked")
+        late = sb.tile([P, 3, 8], F32, name="late", tag="xq", align_bytes=64)
         load_columns(late, (gn, sl, th), nc.sync)
         gn_t, sl_t, th_t = late[:, 0, 0:4], late[:, 1, 0:4], late[:, 2, 0:4]
         w3_d = deal_words_vector("w3_d")
@@ -177,10 +176,9 @@ def tile_picked_hmixeosekd_none_po_kernel(
         zb = sb.tile([P, 4, S], BF16, name="zb")
         part = sb.tile([P, 4, S], F32, name="part")
         twice = [1, 2, 3] if DIVIDED else [0, 1, 2, 3]
-        for l in range(2):
-            nc.scalar.activation(ln[:, twice[0], l, :], ea[twice[0]][:, l, :], ACT.Ln, bias=0.25)
-        for t in twice[1:]:
-            nc.scalar.activation(ln[:, t, :, :], ea[t][:], ACT.Ln, bias=0.25)
+        for t in twice:
+            for l in range(2):
+                nc.scalar.activation(ln[:, t, l, :], ea[t][:, l, :], ACT.Ln, bias=0.25)
         if DIVIDED:
             nc.scalar.activation(ln[:, 0, 0, :], ratio[:], ACT.Ln)
         for t in twice:
@@ -225,10 +223,12 @@ def tile_picked_hmixeosekd_none_po_kernel(
             if t in SCALAR_TILES:
                 nc.scalar.activation(hs[t][:], h_bank[t][:], ACT.Copy, scale=-0.5)
             else:
-                nc.vector.tensor_scalar(hs[t][:, :S], h_bank[t][:], -0.5, None, ALU.mult)
+                nc.vector.tensor_scalar(hs[t][:], h_bank[t][:], -0.5, None, ALU.mult)
             nc.vector.tensor_tensor(prod[:, t, :], h_bank[t][:], sg[:, t, :], ALU.mult)
             if t not in SCALAR_TILES:
-                nc.vector.tensor_tensor(res[:, t, :], hs[t][:].indirect(n4_t[:]), prod[:, t, :], ALU.add)
+                for h in range(2):
+                    looked = hs[t][:].indirect(n4_t[:, list_halves[h]])
+                    nc.vector.tensor_tensor(res[:, t, halves[h]], looked, prod[:, t, halves[h]], ALU.add)
                 nc.sync.dma_start(out_rows[:, t, :], res[:, t, :])
         for h in range(2):
             for t in SCALAR_TILES:

from contextlib import ExitStack

import concourse.mybir as mybir

F32 = mybir.dt.float32
BF16 = mybir.dt.bfloat16
I32 = mybir.dt.int32
U32 = mybir.dt.uint32
U16 = mybir.dt.uint16
U8 = mybir.dt.uint8
FP8X4 = mybir.dt.float8_e4m3fn_x4
FP4X4 = mybir.dt.float4_e2m1fn_x4
ALU = mybir.AluOpType
ACT = mybir.ActivationFunctionType

P = 128
T = 2048
S = 512
HALF = 256
F32_LOWEST = -3.4028234663852886e38
FLOPS = 3 * 2 * 512 * 512 * 512
DIVIDED = True
SCALAR_TILES = (2, 3)


def tile_picked_hmixeosekd_none_po_kernel(
    tc, x_words, x_scales, w1_words, w1_scales, tau, tau2, gn, w2_words, w2_scales, w3_words, w3_scales,
    tab, sl, th, offs, n1, n2, two, n3, n4, out_0, out_1, out_2,
):
    nc = tc.nc
    with ExitStack() as ctx:
        lists = ctx.enter_context(tc.tile_pool(name="lists", bufs=1))
        sb = ctx.enter_context(tc.tile_pool(name="sb", bufs=1))
        ps = ctx.enter_context(tc.psum_pool(name="ps", bufs=1))
        halves = [slice(h * HALF, (h + 1) * HALF) for h in range(2)]
        list_halves = [slice(h * HALF // 16, (h + 1) * HALF // 16) for h in range(2)]

        def load_list(name, src):
            tile = lists.tile([P, S // 16], U16, name=name)
            nc.sync.dma_start(tile[:], src)
            return tile

        def load_columns(tile, srcs, queue):
            for i, src in enumerate(srcs):
                queue.dma_start(tile[:, i, 0:4], src.rearrange("(p t) o -> p (t o)", t=4))

        def load_scale_rows(src, queues):
            for r in range(4):
                queues[r].dma_start(ws_raw[r:P:32, :].bitcast(I32), src[0, r:16:4, :].bitcast(I32))

        def deal_scales(name):
            dealt = sb.tile([P, S], U8, name=name, align_bytes=64)
            nc.vector.tensor_copy(
                out=dealt[:].rearrange("p (t m) -> p t m", t=4),
                in_=ws_raw[:].rearrange("p (m t) -> p t m", t=4),
            )
            return dealt

        def deal_words_vector(name):
            dealt = sb.tile([P, 2 * S], U8, name=name, align_bytes=64)
            nc.vector.tensor_copy(
                out=dealt[:].rearrange("p (t m b) -> p t m b", t=4, b=2),
                in_=ww_raw[:].rearrange("p (m t b) -> p t m b", t=4, b=2),
            )
            return dealt

        def gather_scales(name, offsets, queues):
            picked = sb.tile([P, S], U8, name=name + "_picked", tag="picked")
            nc.vector.tensor_copy(picked[:], xs_win[:].indirect(offsets[:]))
            plane = sb.tile([P, S], U8, name=name + "_plane", align_bytes=64)
            nc.vector.tensor_copy(plane[:].bitcast(I32), picked[:].bitcast(I32))
            for r in range(1, 4):
                queues[r - 1].dma_start(plane[r:P:32, :].bitcast(I32), picked[8 * r : P : 32, :].bitcast(I32))
            return plane

        xs_win = sb.tile([P, T], U8, name="xs_win")
        nc.gpsimd.memset(xs_win[:].bitcast(I32), 0)
        offs_t = load_list("offs_t", offs)
        nc.scalar.dma_start(xs_win[0:P:8, :].bitcast(I32), x_scales[0].bitcast(I32))
        n1_t = load_list("n1_t", n1)
        n2_t = load_list("n2_t", n2)
        two_t = load_list("two_t", two)
        n3_t = load_list("n3_t", n3)
        n4_t = load_list("n4_t", n4)
        xw_win = sb.tile([P, T], I32, name="xw_win")
        nc.sync.dma_start(xw_win[:], x_words[0].rearrange("p n t -> p (n t)").bitcast(I32))
        ww_raw = sb.tile([P, 2 * S], U8, name="ww_raw")
        nc.gpsimd.dma_start(ww_raw[:].bitcast(I32), w1_words[0].bitcast(I32))
        ws_raw = sb.tile([P, S], U8, name="ws_raw")
        nc.gpsimd.memset(ws_raw[:].bitcast(I32), 0)
        load_scale_rows(w1_scales, [nc.sync] * 4)
        rates = sb.tile([P, 2, 8], F32, name="rates")
        load_columns(rates, (tau, tau2), nc.gpsimd)

        xs_plane = gather_scales("xs", offs_t, [nc.sync] * 3)
        w1_d = sb.tile([P, 2 * S], U8, name="w1_d", align_bytes=64)
        nc.scalar.copy(
            out=w1_d[:].bitcast(U16).rearrange("p (t m) -> p t m", t=4),
            in_=ww_raw[:].bitcast(U16).rearrange("p (m t) -> p t m", t=4),
        )
        w1_s = deal_scales("w1_s")
        xq = sb.tile([P, S], U32, name="xq", align_bytes=64)
        for h in range(2):
            nc.vector.tensor_copy(xq[:, halves[h]], xw_win[:].bitcast(U32).indirect(offs_t[:, list_halves[h]]))


        def mx(out, w_d, w_s, t, rhs, rhs_s, start, stop):
            nc.tensor.matmul_mx(
                out=out, lhsT=w_d[:, 256 * t : 256 * (t + 1)].bitcast(FP4X4), lhsT_scale=w_s[:, P * t : P * (t + 1)],
                rhs=rhs.bitcast(FP8X4), rhs_scale=rhs_s, start=start, stop=stop,
            )

        wide = [sb.tile([P, 2 * S], F32, name="wide%d" % t) for t in range(4)]
        hs = [sb.tile([P, S], F32, name="hs%d" % t) for t in range(4)]
        for tile in wide:
            nc.gpsimd.memset(tile[:, S:], 0.0)
        bias_t = []
        for t in range(4):
            bank = ps.tile([P, S], F32, name="y_bank%d" % t)
            if t == 0:
                for cols in halves:
                    mx(bank[:, cols], w1_d, w1_s, t, xq[:, cols], xs_plane[:, cols], True, True)
            else:
                mx(bank[:], w1_d, w1_s, t, xq[:], xs_plane[:], True, True)
            top = sb.tile([P, 1], F32, name="top%d" % t)
            nc.vector.tensor_scalar(wide[t][:, :S], bank[:], 1.0, F32_LOWEST, ALU.mult, ALU.max, accum_out=top[:])
            bias = sb.tile([P, 2], F32, name="bias%d" % t)
            nc.vector.tensor_scalar(bias[:], rates[:, :, t], top[:], -1.0, ALU.mult, ALU.mult)
            bias_t.append(bias)

        ea = [sb.tile([P, 2, S], F32, name="ea%d" % t) for t in range(4)]
        for t in range(4):
            for l, lst in ((1, n2_t), (0, n1_t)):
                nc.scalar.activation(
                    ea[t][:, l, :], wide[t][:].indirect(lst[:]),
                    ACT.Exp, bias=bias_t[t][:, l : l + 1], scale=rates[:, l, t : t + 1],
                )

        x2s_plane = gather_scales("x2s", two_t, [nc.sync] * 3)
        nc.sync.dma_start(ww_raw[:].bitcast(I32), w3_words[0].bitcast(I32))
        load_scale_rows(w3_scales, [nc.sync] * 4)
        late = sb.tile([P, 3, 8], F32, name="late", tag="xq", align_bytes=64)
        load_columns(late, (gn, sl, th), nc.sync)
        gn_t, sl_t, th_t = late[:, 0, 0:4], late[:, 1, 0:4], late[:, 2, 0:4]
        w3_d = deal_words_vector("w3_d")
        w3_s = deal_scales("w3_s")
        nc.sync.dma_start(ww_raw[:].bitcast(I32), w2_words[0].bitcast(I32))
        load_scale_rows(w2_scales, [nc.sync] * 4)
        ratio = sb.tile([P, S], F32, name="ratio")
        if DIVIDED:
            below = sb.tile([P, S], F32, name="below")
            inverse = sb.tile([P, S], F32, name="inverse")
            nc.vector.tensor_scalar(below[:], ea[0][:, 1, :], 0.25, None, ALU.add)
            nc.vector.reciprocal(inverse[:], below[:])
        x2q = sb.tile([P, S], U32, name="x2q", align_bytes=64)
        nc.vector.tensor_copy(x2q[:], xw_win[:].bitcast(U32).indirect(two_t[:]))
        if DIVIDED:
            nc.vector.scalar_tensor_tensor(ratio[:], ea[0][:, 0, :], 0.25, inverse[:], ALU.add, ALU.mult)
        gains = sb.tile([P, 2, 4], F32, name="gains")
        nc.vector.tensor_scalar(gains[:, 0, :], gn_t, 0.5, None, ALU.mult)
        nc.vector.tensor_scalar(gains[:, 1, :], gn_t, -1.0, None, ALU.mult)
        yg = sb.tile([P, 4, S], F32, name="yg")
        for t in range(4):
            nc.vector.tensor_scalar(yg[:, t, :], wide[t][:, :S], gains[:, 0, t : t + 1], None, ALU.mult)
        w2_d = deal_words_vector("w2_d")
        w2_s = deal_scales("w2_s")
        sg_bias = sb.tile([P, 4], F32, name="sg_bias")
        nc.vector.scalar_tensor_tensor(sg_bias[:], sl_t, -1.0, th_t, ALU.mult, ALU.mult)
        h_bank = [ps.tile([P, S], F32, name="h_bank%d" % t) for t in range(4)]
        for t in range(4):
            mx(h_bank[t][:], w3_d, w3_s, t, x2q[:], x2s_plane[:], True, False)
        for t in range(4):
            nc.sync.dma_start(wide[t][:, :S], tab.rearrange("(p t) c -> p t c", t=4)[:, t, :])

        ln = sb.tile([P, 4, 2, S], F32, name="ln")
        zb = sb.tile([P, 4, S], BF16, name="zb")
        part = sb.tile([P, 4, S], F32, name="part")
        twice = [1, 2, 3] if DIVIDED else [0, 1, 2, 3]
        for t in twice:
            for l in range(2):
                nc.scalar.activation(ln[:, t, l, :], ea[t][:, l, :], ACT.Ln, bias=0.25)
        if DIVIDED:
            nc.scalar.activation(ln[:, 0, 0, :], ratio[:], ACT.Ln)
        for t in twice:
            nc.vector.scalar_tensor_tensor(part[:, t, :], ln[:, t, 0, :], gn_t[:, t : t + 1], yg[:, t, :], ALU.mult, ALU.add)
            nc.vector.scalar_tensor_tensor(zb[:, t, :], ln[:, t, 1, :], gains[:, 1, t : t + 1], part[:, t, :], ALU.mult, ALU.add)
        if DIVIDED:
            nc.vector.scalar_tensor_tensor(zb[:, 0, :], ln[:, 0, 0, :], gn_t[:, 0:1], yg[:, 0, :], ALU.mult, ALU.add)

        def interleave(engine_copy, dst, src):
            engine_copy(
                out=dst.rearrange("p (c i) t -> p c t i", i=4), in_=src.rearrange("p t (c i) -> p c t i", i=4)
            )

        zi = [sb.tile([P, HALF, 4], BF16, name="zi%d" % h, align_bytes=64) for h in range(2)]
        zq = [sb.tile([P, HALF], U32, name="zq%d" % h, align_bytes=64) for h in range(2)]
        zs = [sb.tile([P, HALF], U8, name="zs%d" % h, align_bytes=64) for h in range(2)]
        for h in range(2):
            interleave(nc.vector.tensor_copy, zi[h][:], zb[:, :, halves[h]])
        for h in range(2):
            nc.vector.quantize_mx(out=zq[h][:].bitcast(FP8X4), scales=zs[h][:], in_=zi[h][:].rearrange("p c t -> p (c t)"))
        for t in range(4):
            for h in range(2):
                mx(h_bank[t][:, halves[h]], w2_d, w2_s, t, zq[h][:], zs[h][:], False, h == 1)

        sg = sb.tile([P, 4, S], F32, name="sg", tag="ratio" if DIVIDED else "ea3")
        for t in range(4):
            nc.scalar.activation(
                sg[:, t, :], wide[t][:].indirect(n3_t[:]),
                ACT.Sigmoid, bias=sg_bias[:, t : t + 1], scale=sl_t[:, t : t + 1],
            )

        prod = sb.tile([P, 4, S], F32, name="prod")
        fetched = sb.tile([P, 4, S], F32, name="fetched")
        res = sb.tile([P, 4, S], F32, name="res")
        rb = [sb.tile([P, HALF, 4], BF16, name="rb%d" % h, align_bytes=64) for h in range(2)]
        oq = sb.tile([P, S], U32, name="oq", align_bytes=64)
        osc = sb.tile([P, S], U8, name="osc", align_bytes=64)
        out_rows = out_0.rearrange("(p t) c -> p t c", t=4)
        out_words = out_1[0].rearrange("p c r -> p (c r)").bitcast(I32)

        for t in range(4):
            if t in SCALAR_TILES:
                nc.scalar.activation(hs[t][:], h_bank[t][:], ACT.Copy, scale=-0.5)
            else:
                nc.vector.tensor_scalar(hs[t][:], h_bank[t][:], -0.5, None, ALU.mult)
            nc.vector.tensor_tensor(prod[:, t, :], h_bank[t][:], sg[:, t, :], ALU.mult)
            if t not in SCALAR_TILES:
                for h in range(2):
                    looked = hs[t][:].indirect(n4_t[:, list_halves[h]])
                    nc.vector.tensor_tensor(res[:, t, halves[h]], looked, prod[:, t, halves[h]], ALU.add)
                nc.sync.dma_start(out_rows[:, t, :], res[:, t, :])
        for h in range(2):
            for t in SCALAR_TILES:
                nc.scalar.activation(fetched[:, t, halves[h]], hs[t][:].indirect(n4_t[:, list_halves[h]]), ACT.Copy)
                nc.vector.tensor_tensor(res[:, t, halves[h]], fetched[:, t, halves[h]], prod[:, t, halves[h]], ALU.add)
        for t in SCALAR_TILES:
            nc.sync.dma_start(out_rows[:, t, :], res[:, t, :])
        interleave(nc.scalar.copy, rb[0][:], res[:, :, halves[0]])
        interleave(nc.vector.tensor_copy, rb[1][:], res[:, :, halves[1]])
        for h in (1, 0):
            nc.vector.quantize_mx(
                out=oq[:, halves[h]].bitcast(FP8X4), scales=osc[:, halves[h]], in_=rb[h][:].rearrange("p c t -> p (c t)")
            )
            nc.sync.dma_start(out_words[:, halves[h]], oq[:, halves[h]].bitcast(I32))
        for q in range(4):
            queue = nc.scalar if q % 2 == 0 else nc.sync
            queue.dma_start(out_2[0, 4 * q : 4 * q + 4, :].bitcast(I32), osc[32 * q : 32 * q + 4, :].bitcast(I32))
